import numpy as np
import ml_dtypes


def mxq(x, axis, fmt="e4m3"):
    dtype, down = {"e4m3": (ml_dtypes.float8_e4m3fn, 7), "e5m2": (ml_dtypes.float8_e5m2, 14)}[fmt]
    v = np.moveaxis(np.asarray(x, np.float32).astype(ml_dtypes.bfloat16).astype(np.float64), axis, -1)
    blocks = v.reshape(v.shape[:-1] + (-1, 32))
    amax = np.abs(blocks).max(-1, keepdims=True)
    byte = np.maximum(np.where(amax > 0, np.frexp(amax)[1] - 1 + 127, 0) - down, 1)
    scale = np.exp2(byte - 127.0)
    codes = (blocks / scale).astype(np.float32).astype(dtype).astype(np.float64)
    return np.moveaxis((codes * scale).reshape(v.shape), -1, axis)


WIDE = False


def mx_kscale(k):
    if not WIDE:
        return np.ones(k)
    levels = np.array([10, -10, 5, -5, 0])
    if k % 512:
        return np.exp2(np.random.permutation(np.resize(levels, k // 32))).repeat(32)
    a = np.empty((k // 512, 16))
    for p in range(k // 512):
        a[p, :8] = np.random.permutation(np.resize(levels, 8))
        for g in range(8):
            far = levels[np.abs(levels - a[p, g]) >= 10]
            a[p, g + 8] = far[np.random.randint(len(far))]
    return np.exp2(a.ravel()).repeat(32)


def f64(x):
    return np.asarray(x).astype(np.float64)


def striped(idx):
    return np.tile(idx.reshape(-1, 16).T, (8, 1)).astype(np.uint16)


def unstriped(offs):
    return offs[:16].T.reshape(-1).astype(np.int64)


def striped8(idx):
    return np.concatenate([x.reshape(-1, 16).T for x in idx]).astype(np.uint16)


def runs(offs, k):
    lists = np.stack([offs[16 * r : 16 * r + 16].T.reshape(-1) for r in range(8)]).astype(np.int64)
    return lists[np.arange(k) % 512 // 64]


def pack_weight(w):
    k, n = w.shape
    w = f64(np.asarray(w, np.float32).astype(ml_dtypes.bfloat16)).reshape(k // 32, 32, n)
    amax = np.abs(w).max(1)
    byte = np.clip(np.where(amax > 0, np.frexp(amax)[1] - 1 + 127 - 7, 1), 1, 254)
    scaled = (w * np.exp2(127.0 - byte)[:, None, :]).reshape(k, n).astype(np.float32)
    words = np.ascontiguousarray(scaled.reshape(k // 512, 128, 4, n).transpose(0, 1, 3, 2)).astype(ml_dtypes.float8_e4m3fn).view(np.uint8)
    return words, np.ascontiguousarray(byte.astype(np.uint8).reshape(k // 512, 16, n))


def unpack_weight(words, scales):
    g, p, n, _ = words.shape
    vals = np.ascontiguousarray(words).view(ml_dtypes.float8_e4m3fn).astype(np.float64) * np.repeat(np.exp2(scales.astype(np.float64) - 127.0), 8, axis=1)[..., None]
    return vals.transpose(0, 1, 3, 2).reshape(g * 512, n)


def sigmoid(v):
    return 1.0 / (1.0 + np.exp(-np.maximum(v, -700.0)))


K, T, S, V, N, H = 512, 2048, 512, 256, 512, 512


def setup_inputs():
    n = np.random.standard_normal
    s = mx_kscale(K)[:, None]
    u = mx_kscale(S)
    packed_xT = pack_weight(n((K, T)) * s)
    return {
        "x_words": packed_xT[0],
        "x_scales": packed_xT[1],
        "wa": (n((K, H)) / np.sqrt(K) / s).astype(np.float32),
        "gt": (np.random.uniform(0.5, 1.5, (S, 1)) * u[:, None]).astype(np.float32),
        "w1": (n((S, N)) / np.sqrt(S) / u[:, None]).astype(np.float32),
        "offs": striped(np.random.permutation(T)[:S]),
        "fa": striped8(np.stack([np.random.permutation(H)[:V] for _ in range(8)])),
        "fb": striped8(np.stack([np.random.permutation(H)[:V] for _ in range(8)])),
    }


def reference(x_words, x_scales, wa, gt, w1, offs, fa, fb):
    xq = unpack_weight(x_words, x_scales)[:, unstriped(offs)]
    y = xq.T @ mxq(f64(wa), 0, "e4m3")
    z = f64(gt) * ((y[np.arange(S)[:, None], runs(fa, S)]) * (sigmoid(y[np.arange(S)[:, None], runs(fb, S)])))
    return mxq(f64(w1), 0, "e4m3").T @ mxq(z, 0, "e4m3")

from contextlib import ExitStack

import concourse.mybir as mybir

K, T, S, V, N, H = 512, 2048, 512, 256, 512, 512
FLOPS = 2 * K * S * H + 2 * S * N * V

F32 = mybir.dt.float32
BF16 = mybir.dt.bfloat16
I32 = mybir.dt.int32
U32 = mybir.dt.uint32
U16 = mybir.dt.uint16
U8 = mybir.dt.uint8
FP8X4 = mybir.dt.float8_e4m3fn_x4
MULT = mybir.AluOpType.mult
SIGMOID = mybir.ActivationFunctionType.Sigmoid

P = 128
PACK = 4
HALF = 256


def interleave(copy, grouped, raw, c0, c1):
    copy(
        out=grouped[:, c0:c1, :].rearrange("p (c i) j -> p c j i", i=4),
        in_=raw[:, :, c0:c1].rearrange("p j (c i) -> p c j i", i=4),
    )


def tile_picked_featglu_none_p_kernel(tc, x_words, x_scales, wa, gt, w1, offs, fa, fb, out):
    nc = tc.nc
    with ExitStack() as ctx:
        keep = ctx.enter_context(tc.tile_pool(name="keep", bufs=1))
        psum = ctx.enter_context(tc.psum_pool(name="psum", bufs=1))

        offs_t = keep.tile([P, S // 16], U16, name="offs_t")
        fa_t = keep.tile([P, V // 16], U16, name="fa_t")
        fb_t = keep.tile([P, V // 16], U16, name="fb_t")
        xw = keep.tile([P, T], U32, name="xw", tag="slot_xw", align_bytes=64)
        xs = keep.tile([P, T], U8, name="xs", tag="slot_xs", align_bytes=64)
        gt_t = keep.tile([P, PACK], F32, name="gt_t")
        warm = keep.tile([P, 1], F32, name="warm")
        w1_raw = [keep.tile([P, PACK, HALF], F32, name=f"w1_raw{h}", align_bytes=64) for h in range(2)]
        wa_raw = [keep.tile([P, PACK, HALF], F32, name=f"wa_raw{h}", tag=f"slot_raw{h}", align_bytes=64) for h in range(2)]
        warm_out = keep.tile([P, 1], F32, name="warm_out")

        nc.vector.memset(xs[:].bitcast(I32), 0)

        def rows(w, h):
            return w[:, h * HALF : (h + 1) * HALF].rearrange("(p j) n -> p j n", j=PACK)

        nc.sync.dma_start(offs_t[:], offs)
        nc.sync.dma_start(fb_t[:], fb)
        for q in range(4):
            nc.sync.dma_start(xs[32 * q : 32 * q + 4, :].bitcast(I32), x_scales[0, 4 * q : 4 * q + 4, :].bitcast(I32))
        nc.gpsimd.memset(warm[:], 0.0)
        nc.scalar.dma_start(wa_raw[0][:], rows(wa, 0))
        nc.scalar.activation(warm_out[:], warm[:], SIGMOID)
        nc.sync.dma_start(xw[:].bitcast(I32), x_words[0].rearrange("p n j -> p (n j)").bitcast(I32))
        nc.sync.dma_start(wa_raw[1][:], rows(wa, 1))
        nc.sync.dma_start(w1_raw[0][:], rows(w1, 0))
        nc.sync.dma_start(fa_t[:], fa)
        nc.sync.dma_start(w1_raw[1][:], rows(w1, 1))
        nc.gpsimd.dma_start(gt_t[:], gt.rearrange("(p j) o -> p (j o)", j=PACK))

        def operand(name, bf_tag=None, codes_tag=None, width=HALF):
            grouped = keep.tile([P, width, PACK], BF16, name=name + "_bf", tag=bf_tag or name + "_bf", align_bytes=64)
            codes = keep.tile([P, width], U32, name=name + "_codes", tag=codes_tag or name + "_codes", align_bytes=64)
            scales = keep.tile([P, width], U8, name=name + "_scales", align_bytes=64)
            return grouped, codes, scales

        def quantise(op):
            grouped, codes, scales = op
            nc.vector.quantize_mx(out=codes[:].bitcast(FP8X4), scales=scales[:], in_=grouped[:].rearrange("p n j -> p (n j)"))

        picked_bytes = keep.tile([P, S], U8, name="picked_bytes", tag="slot_picked", align_bytes=64)
        wa_q = [operand("wa0", codes_tag="slot_picked"), operand("wa1", bf_tag="slot_y1")]

        x_sc = keep.tile([P, PACK, P], U8, name="x_sc", align_bytes=64)
        x_cd = keep.tile([P, PACK, P], U32, name="x_cd", tag="slot_xs", align_bytes=64)

        interleave(nc.scalar.copy, wa_q[0][0], wa_raw[0], 0, HALF)
        nc.vector.tensor_copy(picked_bytes[:], xs[:].indirect(offs_t[:]))
        nc.vector.tensor_copy(x_sc[:], picked_bytes[:].rearrange("p (m t) -> p t m", t=PACK))
        quantise(wa_q[0])
        nc.vector.tensor_copy(x_cd[:].rearrange("p t m -> p m t"), xw[:].indirect(offs_t[:]))
        interleave(nc.scalar.copy, wa_q[1][0], wa_raw[1], 0, 144)
        interleave(nc.vector.tensor_copy, wa_q[1][0], wa_raw[1], 144, HALF)
        quantise(wa_q[1])

        y = [keep.tile([P, H], F32, name=f"y{t}", tag="slot_raw1" if t == 0 else f"slot_y{t}", align_bytes=64) for t in range(PACK)]
        gate = [[keep.tile([P, P], F32, name=f"gate{g}{t}", tag=f"slot_gate{(PACK * g + t) % 3}", align_bytes=64) for t in range(PACK)] for g in range(2)]
        prod = [keep.tile([P, PACK, P], F32, name=f"prod{g}", tag=f"slot_prod{g}", align_bytes=64) for g in range(2)]
        w1_q = [operand("w10"), operand("w11", bf_tag="slot_prod0")]
        z_q = [operand(f"z{g}", width=P) for g in range(2)]

        def project(t, h, copy):
            acc = psum.tile([P, HALF], F32, name=f"acc{t}{h}", tag=f"bank{t % 2 if h == 0 else 2 + t}")
            nc.tensor.matmul_mx(out=acc[:], lhsT=x_cd[:, t, :].bitcast(FP8X4), lhsT_scale=x_sc[:, t, :],
                                rhs=wa_q[h][1][:].bitcast(FP8X4), rhs_scale=wa_q[h][2][:], start=True, stop=True)
            copy(out=y[t][:, h * HALF : (h + 1) * HALF], in_=acc[:])

        def look_up(t, g):
            entries = slice(g * 8, (g + 1) * 8)
            nc.scalar.activation(gate[g][t][:], y[t][:].indirect(fb_t[:, entries]), SIGMOID)
            nc.vector.tensor_tensor(prod[g][:, t, :], y[t][:].indirect(fa_t[:, entries]), gate[g][t][:], MULT)

        def weigh(g):
            nc.vector.tensor_tensor(z_q[g][0][:], prod[g][:].rearrange("p t v -> p v t"), gt_t[:].unsqueeze(1).to_broadcast([P, P, PACK]), MULT)
            quantise(z_q[g])

        def mix(g, h, copy):
            acc = psum.tile([P, 2, P], F32, name=f"res{g}{h}", tag=f"bank{(6 + 2 * g + h) % 8}")
            for c in range(2):
                cols = slice(c * P, (c + 1) * P)
                nc.tensor.matmul_mx(out=acc[:, c, :], lhsT=w1_q[h][1][:, cols].bitcast(FP8X4), lhsT_scale=w1_q[h][2][:, cols],
                                    rhs=z_q[g][1][:].bitcast(FP8X4), rhs_scale=z_q[g][2][:], start=True, stop=True)
            res = keep.tile([P, 2, P], F32, name=f"out{g}{h}")
            copy(out=res[:], in_=acc[:])
            nc.sync.dma_start(out[h * HALF : (h + 1) * HALF, g * P : (g + 1) * P].rearrange("(c p) v -> p c v", p=P), res[:])

        project(0, 0, nc.scalar.copy)
        project(1, 0, nc.scalar.copy)
        project(0, 1, nc.scalar.copy)
        interleave(nc.vector.tensor_copy, w1_q[0][0], w1_raw[0], 0, HALF)
        quantise(w1_q[0])
        project(1, 1, nc.vector.tensor_copy)
        project(2, 0, nc.scalar.copy)
        project(2, 1, nc.vector.tensor_copy)
        look_up(0, 0)
        look_up(1, 0)
        project(3, 0, nc.scalar.copy)
        project(3, 1, nc.vector.tensor_copy)
        look_up(2, 0)
        look_up(3, 0)
        weigh(0)
        for t in range(PACK):
            look_up(t, 1)
        interleave(nc.scalar.copy, w1_q[1][0], w1_raw[1], 0, HALF)
        mix(0, 0, nc.scalar.copy)
        quantise(w1_q[1])
        weigh(1)
        mix(0, 1, nc.scalar.copy)
        mix(1, 0, nc.scalar.copy)
        mix(1, 1, nc.vector.tensor_copy)
